import numpy as np
import ml_dtypes


def mxq(x, axis, fmt="e4m3"):
    dtype, down = {"e4m3": (ml_dtypes.float8_e4m3fn, 7), "e5m2": (ml_dtypes.float8_e5m2, 14)}[fmt]
    v = np.moveaxis(np.asarray(x, np.float32).astype(ml_dtypes.bfloat16).astype(np.float64), axis, -1)
    blocks = v.reshape(v.shape[:-1] + (-1, 32))
    amax = np.abs(blocks).max(-1, keepdims=True)
    byte = np.maximum(np.where(amax > 0, np.frexp(amax)[1] - 1 + 127, 0) - down, 1)
    scale = np.exp2(byte - 127.0)
    codes = (blocks / scale).astype(np.float32).astype(dtype).astype(np.float64)
    return np.moveaxis((codes * scale).reshape(v.shape), -1, axis)


WIDE = False


def mx_kscale(k, group=512):
    if not WIDE:
        return np.ones(k)
    levels = np.array([10, -10, 5, -5, 0])
    if group != 512:
        return np.exp2(np.random.permutation(np.resize(levels, k // group))).repeat(group)
    if k % 512:
        return np.exp2(np.random.permutation(np.resize(levels, k // 32))).repeat(32)
    a = np.empty((k // 512, 16))
    for p in range(k // 512):
        a[p, :8] = np.random.permutation(np.resize(levels, 8))
        for g in range(8):
            far = levels[np.abs(levels - a[p, g]) >= 10]
            a[p, g + 8] = far[np.random.randint(len(far))]
    return np.exp2(a.ravel()).repeat(32)


def f64(x):
    return np.asarray(x).astype(np.float64)


def sigmoid(v):
    return 1.0 / (1.0 + np.exp(-v))


def silu(v):
    return v / (1.0 + np.exp(-v))


def bf(x):
    return np.asarray(x, np.float32).astype(ml_dtypes.bfloat16)


def planes(Y):
    r, m = Y.shape
    b = f64(bf(Y)).reshape(r // 32, 32, m)
    amax = np.abs(b).max(1)
    byte = np.clip(np.where(amax > 0, np.frexp(amax)[1] - 1 + 127 - 7, 1), 1, 254)
    codes = (b * np.exp2(127.0 - byte)[:, None, :]).reshape(r, m).astype(np.float32).astype(ml_dtypes.float8_e4m3fn).view(np.uint8)
    words = codes.reshape(r // 512, 128, 4, m).transpose(0, 1, 3, 2)
    return np.ascontiguousarray(words), np.ascontiguousarray(byte.astype(np.uint8).reshape(r // 512, 16, m))


G, D, M, N = 2, 256, 256, 512


def setup_inputs():
    n = np.random.standard_normal
    s_d = mx_kscale(D, 0)
    return {
        "x": (n((G, D, N)) * s_d[:, None]).astype(np.float32),
        "w1": (n((G, D, M)) / np.sqrt(D) / s_d[:, None]).astype(np.float32),
        "w2": (n((G, D, M)) / np.sqrt(D) / s_d[:, None]).astype(np.float32),
        "sh": (np.random.uniform(0.1, 0.4, (G, M, 1))).astype(np.float32),
        "d0": (np.random.uniform(5.0, 9.0, (G, M, N))).astype(np.float32),
        "dx": (n((G, D, N)) * s_d[:, None]).astype(np.float32),
        "og": (np.random.uniform(0.5, 2.0, (G, M, 1))).astype(np.float32),
        "base": (0.3 * n((G, M, N))).astype(np.float32),
    }


def reference(x, w1, w2, sh, d0, dx, og, base):
    w1q = mxq(f64(w1), 1, "e4m3")
    xq = mxq(f64(x), 1, "e4m3")
    z1 = w1q.transpose(0, 2, 1) @ xq
    dxq = mxq(f64(dx), 1, "e4m3")
    tz1 = w1q.transpose(0, 2, 1) @ dxq
    w2q = mxq(f64(w2), 1, "e4m3")
    z2 = w2q.transpose(0, 2, 1) @ xq
    tz2 = w2q.transpose(0, 2, 1) @ dxq
    q1 = f64(d0) - z1
    xq1 = tz1 * (-1.0)
    xh = (tz2 * sigmoid(z2) * (1.0 + z2 * (1.0 - sigmoid(z2))) - xq1 * f64(sh) * silu(z2) / (q1 * f64(sh) + 1.0)) / (q1 * f64(sh) + 1.0)
    y = xh * f64(og) + f64(base)
    Y = y.reshape(G * M, N)
    words, scales = planes(Y)
    return Y, words, scales

@@ -1,0 +1,277 @@
+from contextlib import ExitStack
+
+import concourse.mybir as mybir
+
+G, D, M, N = 2, 256, 256, 512
+FLOPS = 4 * 2 * G * D * M * N
+
+F32 = mybir.dt.float32
+BF16 = mybir.dt.bfloat16
+U32 = mybir.dt.uint32
+I32 = mybir.dt.int32
+U8 = mybir.dt.uint8
+FP8X4 = mybir.dt.float8_e4m3fn_x4
+ACT = mybir.ActivationFunctionType
+ALU = mybir.AluOpType
+
+P = 128
+PACK = 4
+ROWS = 64
+H = 2
+CHUNK = 256
+NCH = N // CHUNK
+MM_N = 128
+
+
+def tile_rows_pl_tnkernstudent_kernel(tc, x, w1, w2, sh, d0, dx, og, base, out_0, out_1, out_2):
+    nc = tc.nc
+    with ExitStack() as ctx:
+        sb = ctx.enter_context(tc.tile_pool(name="sb", bufs=1))
+        ps = ctx.enter_context(tc.psum_pool(name="ps", bufs=1))
+        ctx.enter_context(tc.manual_schedule())
+
+        def sbt(name, shape, dtype):
+            return sb.tile(shape, dtype, name=name, align_bytes=64)
+
+        def cols(c):
+            return slice(c * CHUNK, (c + 1) * CHUNK)
+
+        def half(t, h):
+            return t[:, h * CHUNK : (h + 1) * CHUNK]
+
+        def by_h(t):
+            return t[:].rearrange("p (h c) -> p h c", h=H)
+
+        raw, grp, codes, scales = {}, {}, {}, {}
+
+        def load_k(name, src):
+            raw[name] = sbt("raw_" + name, [P, PACK, CHUNK], F32)
+            grp[name] = sbt("grp_" + name, [P, CHUNK, PACK], BF16)
+            codes[name] = sbt("codes_" + name, [P, CHUNK], U32)
+            scales[name] = sbt("scales_" + name, [P, CHUNK], U8)
+            nc.sync.dma_start(out=raw[name][:], in_=src)
+
+        def k_first(t):
+            return t.rearrange("g (p j) n -> (g p) j n", j=PACK)
+
+        def load_rows(name, src):
+            t = sbt(name, [P, H, N], F32)
+            nc.sync.dma_start(out=t[:], in_=src.rearrange("(q h) n -> q h n", h=H))
+            return t
+
+        def load_feature(name, src):
+            t = sbt(name, [P, G, H], F32)
+            nc.sync.dma_start(out=t[:], in_=src.rearrange("g (q h) o -> q g (h o)", h=H))
+            return t
+
+        load_k("w2", k_first(w2))
+        load_k("x0", k_first(x)[:, :, cols(0)])
+        load_k("dx0", k_first(dx)[:, :, cols(0)])
+        load_k("w1", k_first(w1))
+        sh_t = load_feature("sh_t", sh)
+        og_t = load_feature("og_t", og)
+        load_k("x1", k_first(x)[:, :, cols(1)])
+        d0_t = [load_rows("d0_0", d0[0])]
+        load_k("dx1", k_first(dx)[:, :, cols(1)])
+        d0_t.append(load_rows("d0_1", d0[1]))
+        base_t = [load_rows("base_%d" % g, base[g]) for g in range(G)]
+
+        def interleave(copy, dst, src):
+            copy(out=dst.rearrange("p (c i) t -> p c t i", i=4), in_=src.rearrange("p t (c i) -> p c t i", i=4))
+
+        def deal(copy, name):
+            copy(
+                out=grp[name][:].rearrange("p (h c i) j -> p c j i h", h=H, i=2),
+                in_=raw[name][:].rearrange("p j (c i h) -> p c j i h", h=H, i=2),
+            )
+
+        def quantize(name):
+            nc.vector.quantize_mx(
+                out=codes[name][:].bitcast(FP8X4), scales=scales[name][:], in_=grp[name][:].rearrange("p c t -> p (c t)")
+            )
+
+        bank = {}
+        for prod in ("z2", "tz2", "z1", "tz1"):
+            for g in range(G):
+                bank[prod, g] = ps.tile([P, H * CHUNK], F32, name="ps_%s_%d" % (prod, g))
+
+        def product(prod, w, a, groups):
+            for h in range(H):
+                for n0 in range(0, CHUNK, MM_N):
+                    for g in groups:
+                        rows = slice(g * ROWS, (g + 1) * ROWS)
+                        wc = slice(h * P, (h + 1) * P)
+                        ac = slice(n0, n0 + MM_N)
+                        nc.tensor.matmul_mx(
+                            out=bank[prod, g][:, h * CHUNK + n0 : h * CHUNK + n0 + MM_N],
+                            lhsT=codes[w][rows, wc].bitcast(FP8X4),
+                            lhsT_scale=scales[w][rows, wc],
+                            rhs=codes[a][rows, ac].bitcast(FP8X4),
+                            rhs_scale=scales[a][rows, ac],
+                            start=True,
+                            stop=True,
+                        )
+
+        units = [(g, c) for c in range(NCH) for g in range(G)]
+        tq, tt, tz, ta, tn, tb, tr, ty = [], [], [], [], [], [], [], []
+        for u in range(len(units)):
+            for lst, nm in ((tq, "q"), (tt, "t"), (tz, "z"), (ta, "a"), (tn, "n"), (tb, "b"), (tr, "r"), (ty, "y")):
+                lst.append(sbt("%s_%d" % (nm, u), [P, H * CHUNK], F32))
+
+        one = sbt("one", [P, 1], F32)
+        sh_sq = sbt("sh_sq", [P, G, H], F32)
+        sh_fix = sbt("sh_fix", [P, G, H], F32)
+        sh_safe = sbt("sh_safe", [P, G, H], F32)
+        sh_inv = sbt("sh_inv", [P, G, H], F32)
+        gain0 = sbt("gain0", [P, G, H], F32)
+        gain = sbt("gain", [P, G, H], F32)
+        nc.gpsimd.memset(one[:], 1.0)
+
+        def small_constants():
+            nc.gpsimd.tensor_tensor(out=sh_sq[:], in0=sh_t[:], in1=sh_t[:], op=ALU.mult)
+            nc.gpsimd.tensor_scalar(out=sh_fix[:], in0=sh_sq[:], scalar1=2.0**-120, scalar2=2.0**-59, op0=ALU.is_lt, op1=ALU.mult)
+            nc.gpsimd.tensor_tensor(out=sh_safe[:], in0=sh_t[:], in1=sh_fix[:], op=ALU.add)
+            nc.gpsimd.tensor_tensor(out=gain0[:], in0=sh_safe[:], in1=og_t[:], op=ALU.mult)
+            nc.gpsimd.tensor_scalar(out=gain[:], in0=gain0[:], scalar1=0.5, scalar2=0.0, op0=ALU.mult, op1=ALU.add)
+
+        def act_q(u):
+            nc.scalar.activation(out=tq[u][:], in_=bank["z2", units[u][0]][:], func=ACT.Silu, scale=-1.0)
+
+        def act_z(u):
+            nc.scalar.copy(out=tz[u][:], in_=bank["z2", units[u][0]][:])
+
+        def act_t(u):
+            nc.scalar.activation(out=tt[u][:], in_=bank["z2", units[u][0]][:], func=ACT.Tanh, scale=0.5)
+
+        def vec_a(u):
+            nc.vector.scalar_tensor_tensor(
+                out=ta[u][:], in0=tq[u][:], scalar=1.0, in1=bank["tz2", units[u][0]][:], op0=ALU.subtract, op1=ALU.mult
+            )
+
+        def vec_n(u):
+            g, c = units[u]
+            nc.vector.tensor_tensor(out=by_h(tn[u]), in0=d0_t[g][:, :, cols(c)], in1=by_h(bank["z1", g]), op=ALU.subtract)
+
+        def vec_b(u):
+            nc.vector.tensor_tensor(out=tb[u][:], in0=tz[u][:], in1=bank["tz1", units[u][0]][:], op=ALU.mult)
+
+        def vec_m(u):
+            g = units[u][0]
+            for h in range(H):
+                nc.vector.scalar_tensor_tensor(
+                    out=half(ta[u], h), in0=half(tn[u], h), scalar=sh_inv[:, g, h : h + 1], in1=half(ta[u], h),
+                    op0=ALU.add, op1=ALU.mult,
+                )
+
+        def pool_d(u):
+            nc.gpsimd.tensor_tensor(out=tb[u][:], in0=tb[u][:], in1=ta[u][:], op=ALU.subtract)
+
+        def vec_d(u):
+            for h in range(H):
+                nc.vector.tensor_tensor(out=half(tb[u], h), in0=half(tb[u], h), in1=half(ta[u], h), op=ALU.subtract)
+
+        vcopy, scopy = nc.vector.tensor_copy, nc.scalar.copy
+
+        deal(vcopy, "w2")
+        quantize("w2")
+        interleave(vcopy, grp["x0"][:], raw["x0"][:])
+        quantize("x0")
+        product("z2", "w2", "x0", (0, 1))
+        interleave(vcopy, grp["dx0"][:], raw["dx0"][:])
+        quantize("dx0")
+        product("tz2", "w2", "dx0", (0, 1))
+        for h in range(H):
+            nc.gpsimd.tensor_scalar(
+                out=grp["w1"][:, h * P : (h + 1) * P, :],
+                in0=raw["w1"][:].rearrange("p j (q h) -> p h q j", h=H)[:, h],
+                scalar1=1.0, scalar2=0.0, op0=ALU.mult, op1=ALU.add,
+            )
+        small_constants()
+        for step in (act_q, act_z, act_t):
+            step(0)
+            step(1)
+        vec_a(0)
+        vec_a(1)
+        quantize("w1")
+        product("z1", "w1", "x0", (0, 1))
+        product("tz1", "w1", "dx0", (0, 1))
+        interleave(vcopy, grp["x1"][:], raw["x1"][:])
+        nc.vector.reciprocal(out=sh_inv[:], in_=sh_safe[:])
+        vec_n(0)
+        quantize("x1")
+        product("z2", "w2", "x1", (0, 1))
+        vec_b(0)
+        interleave(scopy, grp["dx1"][:], raw["dx1"][:])
+        product("z1", "w1", "x1", (0,))
+        act_q(2)
+        act_z(2)
+        act_q(3)
+        act_z(3)
+        act_t(2)
+        act_t(3)
+        vec_m(0)
+        pool_d(0)
+        vec_n(1)
+        vec_b(1)
+        quantize("dx1")
+        product("tz2", "w2", "dx1", (0, 1))
+        product("tz1", "w1", "dx1", (0,))
+        product("z1", "w1", "x1", (1,))
+        product("tz1", "w1", "dx1", (1,))
+        vec_m(1)
+        pool_d(1)
+        for u in (2, 3):
+            vec_a(u)
+            vec_n(u)
+            vec_b(u)
+            vec_m(u)
+            if u == 2:
+                pool_d(u)
+            else:
+                vec_d(u)
+
+        gathered = [sbt("gathered_%d" % c, [P, PACK, CHUNK], F32) for c in range(NCH)]
+        out_rows = out_0.rearrange("(g q h) n -> g q h n", g=G, h=H)
+        for u, (g, c) in enumerate(units):
+            for h in range(H):
+                nc.scalar.activation(
+                    out=half(tr[u], h), in_=half(tn[u], h), func=ACT.Abs_reciprocal_sqrt,
+                    scale=sh_t[:, g, h : h + 1], bias=one[:],
+                )
+            for rep in range(2):
+                for h in range(H):
+                    nc.scalar.activation(out=half(tr[u], h), in_=half(tr[u], h), func=ACT.Square)
+            for h in range(H):
+                nc.vector.scalar_tensor_tensor(
+                    out=half(tt[u], h), in0=half(tt[u], h), scalar=1.0, in1=half(tr[u], h), op0=ALU.add, op1=ALU.mult
+                )
+            for h in range(H):
+                nc.vector.tensor_tensor(out=half(tb[u], h), in0=half(tb[u], h), in1=half(tt[u], h), op=ALU.mult)
+            for h in range(H):
+                nc.vector.scalar_tensor_tensor(
+                    out=half(ty[u], h), in0=half(tb[u], h), scalar=gain[:, g, h : h + 1], in1=base_t[g][:, h, cols(c)],
+                    op0=ALU.mult, op1=ALU.add,
+                )
+                dst = gathered[c][g * ROWS : (g + 1) * ROWS].rearrange("s (b h) c -> s b h c", h=H)
+                nc.sync.dma_start(out=dst[:, :, h, :], in_=half(ty[u], h))
+            nc.sync.dma_start(out=out_rows[g][:, :, cols(c)], in_=by_h(ty[u]))
+
+        y_scales = sbt("y_scales", [P, N], U8)
+        words = out_1[0].rearrange("p n u -> p (n u)").bitcast(I32)
+        for c in range(NCH):
+            y_grp = sbt("y_grp_%d" % c, [P, CHUNK, PACK], BF16)
+            y_codes = sbt("y_codes_%d" % c, [P, CHUNK], U32)
+            if c == 0:
+                interleave(scopy, y_grp[:], gathered[c][:])
+            else:
+                interleave(vcopy, y_grp[:, :176, :], gathered[c][:, :, :176])
+                interleave(scopy, y_grp[:, 176:, :], gathered[c][:, :, 176:])
+            nc.vector.quantize_mx(
+                out=y_codes[:].bitcast(FP8X4), scales=y_scales[:, cols(c)], in_=y_grp[:].rearrange("p c t -> p (c t)")
+            )
+            nc.sync.dma_start(out=words[:, cols(c)], in_=y_codes[:].bitcast(I32))
+        for quad in range(4):
+            queue = nc.scalar if quad % 2 else nc.sync
+            queue.dma_start(
+                out=out_2[0, 4 * quad : 4 * quad + 4, :].bitcast(I32), in_=y_scales[32 * quad : 32 * quad + 4, :].bitcast(I32)
+            )

@@ -61,20 +61,25 @@ def tile_rows_pl_tnkernstudent_kernel(tc, x, w1, w2, sh, d0, dx, og, base, out_0
 
         def load_feature(name, src):
             t = sbt(name, [P, G, H], F32)
-            nc.sync.dma_start(out=t[:], in_=src.rearrange("g (q h) o -> q g (h o)", h=H))
+            nc.scalar.dma_start(out=t[:], in_=src.rearrange("g (q h) o -> q g (h o)", h=H))
             return t
 
+        sh_both = sbt("sh_both", [P, 2, 8], F32)
+        og_t = sbt("og_t", [P, PACK], F32)
+        sh_t = sh_both[:, 0, 0:PACK].rearrange("q (g h) -> q g h", h=H)
+        nc.scalar.dma_start(out=sh_t, in_=sh.rearrange("g (q h) o -> q g (h o)", h=H))
+        nc.scalar.dma_start(out=sh_both[:, 1, 0:PACK], in_=sh.rearrange("g (s u) o -> (g s) (u o)", u=PACK))
+        nc.scalar.dma_start(out=og_t[:], in_=og.rearrange("g (s u) o -> (g s) (u o)", u=PACK))
         load_k("w2", k_first(w2))
         load_k("x0", k_first(x)[:, :, cols(0)])
         load_k("dx0", k_first(dx)[:, :, cols(0)])
         load_k("w1", k_first(w1))
-        sh_t = load_feature("sh_t", sh)
-        og_t = load_feature("og_t", og)
         load_k("x1", k_first(x)[:, :, cols(1)])
         d0_t = [load_rows("d0_0", d0[0])]
         load_k("dx1", k_first(dx)[:, :, cols(1)])
         d0_t.append(load_rows("d0_1", d0[1]))
-        base_t = [load_rows("base_%d" % g, base[g]) for g in range(G)]
+        base_t = sbt("base_t", [P, PACK, N], F32)
+        nc.sync.dma_start(out=base_t[:], in_=k_first(base))
 
         def interleave(copy, dst, src):
             copy(out=dst.rearrange("p (c i) t -> p c t i", i=4), in_=src.rearrange("p t (c i) -> p c t i", i=4))
@@ -113,32 +118,32 @@ def tile_rows_pl_tnkernstudent_kernel(tc, x, w1, w2, sh, d0, dx, og, base, out_0
                         )
 
         units = [(g, c) for c in range(NCH) for g in range(G)]
-        tq, tt, tz, ta, tn, tb, tr, ty = [], [], [], [], [], [], [], []
+        tq, tt, tz, ta, tn, tb, tr = [], [], [], [], [], [], []
         for u in range(len(units)):
-            for lst, nm in ((tq, "q"), (tt, "t"), (tz, "z"), (ta, "a"), (tn, "n"), (tb, "b"), (tr, "r"), (ty, "y")):
+            for lst, nm in ((tq, "q"), (tt, "t"), (tz, "z"), (ta, "a"), (tn, "n"), (tb, "b"), (tr, "r")):
                 lst.append(sbt("%s_%d" % (nm, u), [P, H * CHUNK], F32))
 
         one = sbt("one", [P, 1], F32)
-        sh_sq = sbt("sh_sq", [P, G, H], F32)
-        sh_fix = sbt("sh_fix", [P, G, H], F32)
-        sh_safe = sbt("sh_safe", [P, G, H], F32)
+        sh_sq = sbt("sh_sq", [P, 2, PACK], F32)
+        sh_fix = sbt("sh_fix", [P, 2, PACK], F32)
+        sh_safe = sbt("sh_safe", [P, 2, PACK], F32)
         sh_inv = sbt("sh_inv", [P, G, H], F32)
-        gain0 = sbt("gain0", [P, G, H], F32)
-        gain = sbt("gain", [P, G, H], F32)
+        gain0 = sbt("gain0", [P, PACK], F32)
+        gain = sbt("gain", [P, PACK], F32)
         nc.gpsimd.memset(one[:], 1.0)
 
         def small_constants():
-            nc.gpsimd.tensor_tensor(out=sh_sq[:], in0=sh_t[:], in1=sh_t[:], op=ALU.mult)
+            nc.gpsimd.tensor_tensor(out=sh_sq[:], in0=sh_both[:, :, 0:PACK], in1=sh_both[:, :, 0:PACK], op=ALU.mult)
             nc.gpsimd.tensor_scalar(out=sh_fix[:], in0=sh_sq[:], scalar1=2.0**-120, scalar2=2.0**-59, op0=ALU.is_lt, op1=ALU.mult)
-            nc.gpsimd.tensor_tensor(out=sh_safe[:], in0=sh_t[:], in1=sh_fix[:], op=ALU.add)
-            nc.gpsimd.tensor_tensor(out=gain0[:], in0=sh_safe[:], in1=og_t[:], op=ALU.mult)
+            nc.gpsimd.tensor_tensor(out=sh_safe[:], in0=sh_both[:, :, 0:PACK], in1=sh_fix[:], op=ALU.add)
+            nc.gpsimd.tensor_tensor(out=gain0[:], in0=sh_safe[:, 1, :], in1=og_t[:], op=ALU.mult)
             nc.gpsimd.tensor_scalar(out=gain[:], in0=gain0[:], scalar1=0.5, scalar2=0.0, op0=ALU.mult, op1=ALU.add)
 
         def act_q(u):
             nc.scalar.activation(out=tq[u][:], in_=bank["z2", units[u][0]][:], func=ACT.Silu, scale=-1.0)
 
         def act_z(u):
-            nc.scalar.copy(out=tz[u][:], in_=bank["z2", units[u][0]][:])
+            nc.scalar.activation(out=tz[u][:], in_=bank["z2", units[u][0]][:], func=ACT.Silu)
 
         def act_t(u):
             nc.scalar.activation(out=tt[u][:], in_=bank["z2", units[u][0]][:], func=ACT.Tanh, scale=0.5)
@@ -153,7 +158,14 @@ def tile_rows_pl_tnkernstudent_kernel(tc, x, w1, w2, sh, d0, dx, og, base, out_0
             nc.vector.tensor_tensor(out=by_h(tn[u]), in0=d0_t[g][:, :, cols(c)], in1=by_h(bank["z1", g]), op=ALU.subtract)
 
         def vec_b(u):
-            nc.vector.tensor_tensor(out=tb[u][:], in0=tz[u][:], in1=bank["tz1", units[u][0]][:], op=ALU.mult)
+            nc.vector.scalar_tensor_tensor(
+                out=tb[u][:], in0=bank["tz1", units[u][0]][:], scalar=2.0, in1=tz[u][:], op0=ALU.mult, op1=ALU.mult
+            )
+
+        def vec_g(u):
+            nc.vector.scalar_tensor_tensor(
+                out=ta[u][:], in0=tt[u][:], scalar=1.0, in1=ta[u][:], op0=ALU.add, op1=ALU.mult
+            )
 
         def vec_m(u):
             g = units[u][0]
@@ -167,72 +179,35 @@ def tile_rows_pl_tnkernstudent_kernel(tc, x, w1, w2, sh, d0, dx, og, base, out_0
             nc.gpsimd.tensor_tensor(out=tb[u][:], in0=tb[u][:], in1=ta[u][:], op=ALU.subtract)
 
         def vec_d(u):
-            for h in range(H):
-                nc.vector.tensor_tensor(out=half(tb[u], h), in0=half(tb[u], h), in1=half(ta[u], h), op=ALU.subtract)
+            nc.vector.tensor_tensor(out=tb[u][:], in0=tb[u][:], in1=ta[u][:], op=ALU.subtract)
 
         vcopy, scopy = nc.vector.tensor_copy, nc.scalar.copy
 
-        deal(vcopy, "w2")
-        quantize("w2")
-        interleave(vcopy, grp["x0"][:], raw["x0"][:])
-        quantize("x0")
-        product("z2", "w2", "x0", (0, 1))
-        interleave(vcopy, grp["dx0"][:], raw["dx0"][:])
-        quantize("dx0")
-        product("tz2", "w2", "dx0", (0, 1))
-        for h in range(H):
-            nc.gpsimd.tensor_scalar(
-                out=grp["w1"][:, h * P : (h + 1) * P, :],
-                in0=raw["w1"][:].rearrange("p j (q h) -> p h q j", h=H)[:, h],
-                scalar1=1.0, scalar2=0.0, op0=ALU.mult, op1=ALU.add,
-            )
-        small_constants()
-        for step in (act_q, act_z, act_t):
-            step(0)
-            step(1)
-        vec_a(0)
-        vec_a(1)
-        quantize("w1")
-        product("z1", "w1", "x0", (0, 1))
-        product("tz1", "w1", "dx0", (0, 1))
-        interleave(vcopy, grp["x1"][:], raw["x1"][:])
-        nc.vector.reciprocal(out=sh_inv[:], in_=sh_safe[:])
-        vec_n(0)
-        quantize("x1")
-        product("z2", "w2", "x1", (0, 1))
-        vec_b(0)
-        interleave(scopy, grp["dx1"][:], raw["dx1"][:])
-        product("z1", "w1", "x1", (0,))
-        act_q(2)
-        act_z(2)
-        act_q(3)
-        act_z(3)
-        act_t(2)
-        act_t(3)
-        vec_m(0)
-        pool_d(0)
-        vec_n(1)
-        vec_b(1)
-        quantize("dx1")
-        product("tz2", "w2", "dx1", (0, 1))
-        product("tz1", "w1", "dx1", (0,))
-        product("z1", "w1", "x1", (1,))
-        product("tz1", "w1", "dx1", (1,))
-        vec_m(1)
-        pool_d(1)
-        for u in (2, 3):
-            vec_a(u)
-            vec_n(u)
-            vec_b(u)
-            vec_m(u)
-            if u == 2:
-                pool_d(u)
-            else:
-                vec_d(u)
+        def gcopy(out, in_):
+            nc.gpsimd.tensor_scalar(out=out, in0=in_, scalar1=1.0, scalar2=0.0, op0=ALU.mult, op1=ALU.add)
 
         gathered = [sbt("gathered_%d" % c, [P, PACK, CHUNK], F32) for c in range(NCH)]
-        out_rows = out_0.rearrange("(g q h) n -> g q h n", g=G, h=H)
-        for u, (g, c) in enumerate(units):
+        out_rows = out_0.rearrange("(p u) n -> p u n", u=PACK)
+        ty = [sbt("y_%d" % c, [P, PACK, CHUNK], F32) for c in range(NCH)]
+        y_scales = sbt("y_scales", [P, N], U8)
+        words = out_1[0].rearrange("p n u -> p (n u)").bitcast(I32)
+        y_grp = [sbt("y_grp_%d" % c, [P, CHUNK, PACK], BF16) for c in range(NCH)]
+        y_codes = [sbt("y_codes_%d" % c, [P, CHUNK], U32) for c in range(NCH)]
+
+        def act_r(pair):
+            for u in pair:
+                g = units[u][0]
+                for h in range(H):
+                    nc.scalar.activation(
+                        out=half(tr[u], h), in_=half(tn[u], h), func=ACT.Abs_reciprocal_sqrt,
+                        scale=sh_t[:, g, h : h + 1], bias=one[:],
+                    )
+            for rep in range(2):
+                for u in pair:
+                    nc.scalar.activation(out=tr[u][:], in_=tr[u][:], func=ACT.Square)
+
+        def act_r1(u):
+            g = units[u][0]
             for h in range(H):
                 nc.scalar.activation(
                     out=half(tr[u], h), in_=half(tn[u], h), func=ACT.Abs_reciprocal_sqrt,
@@ -241,35 +216,123 @@ def tile_rows_pl_tnkernstudent_kernel(tc, x, w1, w2, sh, d0, dx, og, base, out_0
             for rep in range(2):
                 for h in range(H):
                     nc.scalar.activation(out=half(tr[u], h), in_=half(tr[u], h), func=ACT.Square)
+
+        def pool_f(u):
+            nc.gpsimd.tensor_tensor(out=tb[u][:], in0=tb[u][:], in1=tr[u][:], op=ALU.mult)
+
+        def vec_f(u):
+            nc.vector.tensor_tensor(out=tb[u][:], in0=tb[u][:], in1=tr[u][:], op=ALU.mult)
+            gather(u, (0, 1))
+
+        def gather(u, hs):
+            g, c = units[u]
+            dst = gathered[c][g * ROWS : (g + 1) * ROWS].rearrange("s (b h) c -> s b h c", h=H)
+            if len(hs) == H:
+                nc.sync.dma_start(out=dst.rearrange("s b h c -> s b (h c)"), in_=tb[u][:])
+            else:
+                nc.sync.dma_start(out=dst[:, :, hs[0], :], in_=half(tb[u], hs[0]))
+
+        def vec_fh(u):
             for h in range(H):
+                nc.vector.tensor_tensor(out=half(tb[u], h), in0=half(tb[u], h), in1=half(tr[u], h), op=ALU.mult)
+                gather(u, (h,))
+
+        def vec_y(c):
+            for u in range(PACK):
                 nc.vector.scalar_tensor_tensor(
-                    out=half(tt[u], h), in0=half(tt[u], h), scalar=1.0, in1=half(tr[u], h), op0=ALU.add, op1=ALU.mult
-                )
-            for h in range(H):
-                nc.vector.tensor_tensor(out=half(tb[u], h), in0=half(tb[u], h), in1=half(tt[u], h), op=ALU.mult)
-            for h in range(H):
-                nc.vector.scalar_tensor_tensor(
-                    out=half(ty[u], h), in0=half(tb[u], h), scalar=gain[:, g, h : h + 1], in1=base_t[g][:, h, cols(c)],
+                    out=ty[c][:, u, :], in0=gathered[c][:, u, :], scalar=gain[:, u : u + 1], in1=base_t[:, u, cols(c)],
                     op0=ALU.mult, op1=ALU.add,
                 )
-                dst = gathered[c][g * ROWS : (g + 1) * ROWS].rearrange("s (b h) c -> s b h c", h=H)
-                nc.sync.dma_start(out=dst[:, :, h, :], in_=half(ty[u], h))
-            nc.sync.dma_start(out=out_rows[g][:, :, cols(c)], in_=by_h(ty[u]))
+                if u % 2:
+                    nc.sync.dma_start(out=out_rows[:, u - 1 : u + 1, cols(c)], in_=ty[c][:, u - 1 : u + 1, :])
 
-        y_scales = sbt("y_scales", [P, N], U8)
-        words = out_1[0].rearrange("p n u -> p (n u)").bitcast(I32)
-        for c in range(NCH):
-            y_grp = sbt("y_grp_%d" % c, [P, CHUNK, PACK], BF16)
-            y_codes = sbt("y_codes_%d" % c, [P, CHUNK], U32)
-            if c == 0:
-                interleave(scopy, y_grp[:], gathered[c][:])
-            else:
-                interleave(vcopy, y_grp[:, :176, :], gathered[c][:, :, :176])
-                interleave(scopy, y_grp[:, 176:, :], gathered[c][:, :, 176:])
+        def planes(c):
             nc.vector.quantize_mx(
-                out=y_codes[:].bitcast(FP8X4), scales=y_scales[:, cols(c)], in_=y_grp[:].rearrange("p c t -> p (c t)")
+                out=y_codes[c][:].bitcast(FP8X4), scales=y_scales[:, cols(c)], in_=y_grp[c][:].rearrange("p c t -> p (c t)")
             )
-            nc.sync.dma_start(out=words[:, cols(c)], in_=y_codes[:].bitcast(I32))
+            nc.sync.dma_start(out=words[:, cols(c)], in_=y_codes[c][:].bitcast(I32))
+
+        small_constants()
+        deal(vcopy, "w2")
+        quantize("w2")
+        interleave(vcopy, grp["x0"][:], raw["x0"][:])
+        nc.vector.reciprocal(out=sh_inv[:].rearrange("q g h -> q (g h)"), in_=sh_safe[:, 0, :])
+        quantize("x0")
+        product("z2", "w2", "x0", (0,))
+        product("z2", "w2", "x0", (1,))
+        interleave(vcopy, grp["dx0"][:], raw["dx0"][:])
+        quantize("dx0")
+        product("tz2", "w2", "dx0", (0,))
+        deal(vcopy, "w1")
+        quantize("w1")
+        product("tz2", "w2", "dx0", (1,))
+        product("z1", "w1", "x0", (0,))
+        product("tz1", "w1", "dx0", (0,))
+        product("z1", "w1", "x0", (1,))
+        product("tz1", "w1", "dx0", (1,))
+        act_q(0)
+        act_q(1)
+        act_t(0)
+        act_z(0)
+        act_t(1)
+        act_z(1)
+        vec_a(0)
+        interleave(vcopy, grp["x1"][:], raw["x1"][:])
+        vec_a(1)
+        quantize("x1")
+        product("z2", "w2", "x1", (0,))
+        product("z2", "w2", "x1", (1,))
+        interleave(scopy, grp["dx1"][:], raw["dx1"][:])
+        vec_g(0)
+        vec_n(0)
+        product("z1", "w1", "x1", (0,))
+        vec_b(0)
+        vec_g(1)
+        vec_m(0)
+        pool_d(0)
+        vec_n(1)
+        vec_b(1)
+        quantize("dx1")
+        product("tz2", "w2", "dx1", (0,))
+        product("tz1", "w1", "dx1", (0,))
+        product("z1", "w1", "x1", (1,))
+        product("tz2", "w2", "dx1", (1,))
+        product("tz1", "w1", "dx1", (1,))
+        act_q(2)
+        act_t(2)
+        act_z(2)
+        act_q(3)
+        act_t(3)
+        act_z(3)
+        vec_m(1)
+        pool_d(1)
+        vec_n(2)
+        vec_a(2)
+        vec_g(2)
+        vec_b(2)
+        vec_m(2)
+        pool_d(2)
+        vec_n(3)
+        vec_a(3)
+        act_r1(0)
+        act_r1(1)
+        act_r1(2)
+        act_r1(3)
+        vec_f(0)
+        vec_g(3)
+        vec_b(3)
+        vec_f(1)
+        vec_m(3)
+        vec_f(2)
+        vec_d(3)
+        vec_fh(3)
+        vec_y(0)
+        interleave(scopy, y_grp[0][:], ty[0][:])
+        vec_y(1)
+        planes(0)
+        interleave(vcopy, y_grp[1][:, :176, :], ty[1][:, :, :176])
+        interleave(scopy, y_grp[1][:, 176:, :], ty[1][:, :, 176:])
+        planes(1)
         for quad in range(4):
             queue = nc.scalar if quad % 2 else nc.sync
             queue.dma_start(

@@ -64,20 +64,26 @@ def tile_rows_pl_tnkernstudent_kernel(tc, x, w1, w2, sh, d0, dx, og, base, out_0
             nc.scalar.dma_start(out=t[:], in_=src.rearrange("g (q h) o -> q g (h o)", h=H))
             return t
 
-        sh_both = sbt("sh_both", [P, 2, 8], F32)
+        sh_t = sbt("sh_t", [P, G, H], F32)
         og_t = sbt("og_t", [P, PACK], F32)
-        sh_t = sh_both[:, 0, 0:PACK].rearrange("q (g h) -> q g h", h=H)
-        nc.scalar.dma_start(out=sh_t, in_=sh.rearrange("g (q h) o -> q g (h o)", h=H))
-        nc.scalar.dma_start(out=sh_both[:, 1, 0:PACK], in_=sh.rearrange("g (s u) o -> (g s) (u o)", u=PACK))
-        nc.scalar.dma_start(out=og_t[:], in_=og.rearrange("g (s u) o -> (g s) (u o)", u=PACK))
         load_k("w2", k_first(w2))
         load_k("x0", k_first(x)[:, :, cols(0)])
         load_k("dx0", k_first(dx)[:, :, cols(0)])
         load_k("w1", k_first(w1))
+        d0_t = {}
+
+        def load_d0(g, c):
+            d0_t[g, c] = sbt("d0_%d_%d" % (g, c), [P, H, CHUNK], F32)
+            nc.sync.dma_start(out=d0_t[g, c][:], in_=d0[g].rearrange("(q h) n -> q h n", h=H)[:, :, cols(c)])
+
         load_k("x1", k_first(x)[:, :, cols(1)])
-        d0_t = [load_rows("d0_0", d0[0])]
+        load_d0(0, 0)
+        load_d0(1, 0)
+        nc.sync.dma_start(out=sh_t[:], in_=sh.rearrange("g (q h) o -> q g (h o)", h=H))
         load_k("dx1", k_first(dx)[:, :, cols(1)])
-        d0_t.append(load_rows("d0_1", d0[1]))
+        load_d0(0, 1)
+        load_d0(1, 1)
+        nc.sync.dma_start(out=og_t[:], in_=og.rearrange("g (s u) o -> (g s) (u o)", u=PACK))
         base_t = sbt("base_t", [P, PACK, N], F32)
         nc.sync.dma_start(out=base_t[:], in_=k_first(base))
 
@@ -124,20 +130,12 @@ def tile_rows_pl_tnkernstudent_kernel(tc, x, w1, w2, sh, d0, dx, og, base, out_0
                 lst.append(sbt("%s_%d" % (nm, u), [P, H * CHUNK], F32))
 
         one = sbt("one", [P, 1], F32)
-        sh_sq = sbt("sh_sq", [P, 2, PACK], F32)
-        sh_fix = sbt("sh_fix", [P, 2, PACK], F32)
-        sh_safe = sbt("sh_safe", [P, 2, PACK], F32)
+        sh_sq = sbt("sh_sq", [P, G, H], F32)
+        sh_fix = sbt("sh_fix", [P, G, H], F32)
+        sh_safe = sbt("sh_safe", [P, G, H], F32)
         sh_inv = sbt("sh_inv", [P, G, H], F32)
-        gain0 = sbt("gain0", [P, PACK], F32)
-        gain = sbt("gain", [P, PACK], F32)
+        sh_half = sbt("sh_half", [P, G, H], F32)
         nc.gpsimd.memset(one[:], 1.0)
-
-        def small_constants():
-            nc.gpsimd.tensor_tensor(out=sh_sq[:], in0=sh_both[:, :, 0:PACK], in1=sh_both[:, :, 0:PACK], op=ALU.mult)
-            nc.gpsimd.tensor_scalar(out=sh_fix[:], in0=sh_sq[:], scalar1=2.0**-120, scalar2=2.0**-59, op0=ALU.is_lt, op1=ALU.mult)
-            nc.gpsimd.tensor_tensor(out=sh_safe[:], in0=sh_both[:, :, 0:PACK], in1=sh_fix[:], op=ALU.add)
-            nc.gpsimd.tensor_tensor(out=gain0[:], in0=sh_safe[:, 1, :], in1=og_t[:], op=ALU.mult)
-            nc.gpsimd.tensor_scalar(out=gain[:], in0=gain0[:], scalar1=0.5, scalar2=0.0, op0=ALU.mult, op1=ALU.add)
 
         def act_q(u):
             nc.scalar.activation(out=tq[u][:], in_=bank["z2", units[u][0]][:], func=ACT.Silu, scale=-1.0)
@@ -155,7 +153,7 @@ def tile_rows_pl_tnkernstudent_kernel(tc, x, w1, w2, sh, d0, dx, og, base, out_0
 
         def vec_n(u):
             g, c = units[u]
-            nc.vector.tensor_tensor(out=by_h(tn[u]), in0=d0_t[g][:, :, cols(c)], in1=by_h(bank["z1", g]), op=ALU.subtract)
+            nc.vector.tensor_tensor(out=by_h(tn[u]), in0=d0_t[g, c][:], in1=by_h(bank["z1", g]), op=ALU.subtract)
 
         def vec_b(u):
             nc.vector.scalar_tensor_tensor(
@@ -220,8 +218,15 @@ def tile_rows_pl_tnkernstudent_kernel(tc, x, w1, w2, sh, d0, dx, og, base, out_0
         def pool_f(u):
             nc.gpsimd.tensor_tensor(out=tb[u][:], in0=tb[u][:], in1=tr[u][:], op=ALU.mult)
 
+        def f_half(u, h):
+            nc.vector.scalar_tensor_tensor(
+                out=half(tb[u], h), in0=half(tb[u], h), scalar=sh_half[:, units[u][0], h : h + 1], in1=half(tr[u], h),
+                op0=ALU.mult, op1=ALU.mult,
+            )
+
         def vec_f(u):
-            nc.vector.tensor_tensor(out=tb[u][:], in0=tb[u][:], in1=tr[u][:], op=ALU.mult)
+            for h in range(H):
+                f_half(u, h)
             gather(u, (0, 1))
 
         def gather(u, hs):
@@ -234,17 +239,31 @@ def tile_rows_pl_tnkernstudent_kernel(tc, x, w1, w2, sh, d0, dx, og, base, out_0
 
         def vec_fh(u):
             for h in range(H):
-                nc.vector.tensor_tensor(out=half(tb[u], h), in0=half(tb[u], h), in1=half(tr[u], h), op=ALU.mult)
+                f_half(u, h)
                 gather(u, (h,))
 
         def vec_y(c):
-            for u in range(PACK):
+            for u in (0, 2, 1, 3):
                 nc.vector.scalar_tensor_tensor(
-                    out=ty[c][:, u, :], in0=gathered[c][:, u, :], scalar=gain[:, u : u + 1], in1=base_t[:, u, cols(c)],
+                    out=ty[c][:, u, :], in0=gathered[c][:, u, :], scalar=og_t[:, u : u + 1], in1=base_t[:, u, cols(c)],
                     op0=ALU.mult, op1=ALU.add,
                 )
-                if u % 2:
-                    nc.sync.dma_start(out=out_rows[:, u - 1 : u + 1, cols(c)], in_=ty[c][:, u - 1 : u + 1, :])
+                if u >= 2:
+                    nc.sync.dma_start(out=out_rows[:, u - 2 :: 2, cols(c)], in_=ty[c][:, u - 2 :: 2, :])
+
+        def vec_y_cols(c, lo, hi):
+            for u in range(PACK):
+                nc.vector.scalar_tensor_tensor(
+                    out=ty[c][:, u, lo:hi], in0=gathered[c][:, u, lo:hi], scalar=og_t[:, u : u + 1],
+                    in1=base_t[:, u, c * CHUNK + lo : c * CHUNK + hi], op0=ALU.mult, op1=ALU.add,
+                )
+            nc.sync.dma_start(out=out_rows[:, :, c * CHUNK + lo : c * CHUNK + hi], in_=ty[c][:, :, lo:hi])
+
+        def planes_cols(c, lo, hi):
+            nc.vector.quantize_mx(
+                out=y_codes[c][:, lo:hi].bitcast(FP8X4), scales=y_scales[:, c * CHUNK + lo : c * CHUNK + hi],
+                in_=y_grp[c][:, lo:hi, :].rearrange("p c t -> p (c t)"),
+            )
 
         def planes(c):
             nc.vector.quantize_mx(
@@ -252,75 +271,70 @@ def tile_rows_pl_tnkernstudent_kernel(tc, x, w1, w2, sh, d0, dx, og, base, out_0
             )
             nc.sync.dma_start(out=words[:, cols(c)], in_=y_codes[c][:].bitcast(I32))
 
-        small_constants()
         deal(vcopy, "w2")
         quantize("w2")
         interleave(vcopy, grp["x0"][:], raw["x0"][:])
-        nc.vector.reciprocal(out=sh_inv[:].rearrange("q g h -> q (g h)"), in_=sh_safe[:, 0, :])
         quantize("x0")
-        product("z2", "w2", "x0", (0,))
-        product("z2", "w2", "x0", (1,))
+        product("z2", "w2", "x0", (0, 1,))
         interleave(vcopy, grp["dx0"][:], raw["dx0"][:])
         quantize("dx0")
-        product("tz2", "w2", "dx0", (0,))
+        product("tz2", "w2", "dx0", (0, 1,))
         deal(vcopy, "w1")
         quantize("w1")
-        product("tz2", "w2", "dx0", (1,))
-        product("z1", "w1", "x0", (0,))
-        product("tz1", "w1", "dx0", (0,))
-        product("z1", "w1", "x0", (1,))
-        product("tz1", "w1", "dx0", (1,))
+        product("z1", "w1", "x0", (0, 1,))
+        product("tz1", "w1", "dx0", (0, 1,))
         act_q(0)
         act_q(1)
         act_t(0)
-        act_z(0)
         act_t(1)
+        act_z(0)
         act_z(1)
-        vec_a(0)
         interleave(vcopy, grp["x1"][:], raw["x1"][:])
-        vec_a(1)
+        vec_a(0)
         quantize("x1")
-        product("z2", "w2", "x1", (0,))
-        product("z2", "w2", "x1", (1,))
+        vec_a(1)
+        product("z2", "w2", "x1", (0, 1,))
+        nc.scalar.activation(out=sh_sq[:], in_=sh_t[:], func=ACT.Square)
         interleave(scopy, grp["dx1"][:], raw["dx1"][:])
         vec_g(0)
         vec_n(0)
-        product("z1", "w1", "x1", (0,))
-        vec_b(0)
         vec_g(1)
+        nc.vector.tensor_scalar(out=sh_fix[:], in0=sh_sq[:], scalar1=2.0**-120, scalar2=2.0**-59, op0=ALU.is_lt, op1=ALU.mult)
+        vec_n(1)
+        product("z1", "w1", "x1", (0, 1,))
+        nc.vector.tensor_tensor(out=sh_safe[:], in0=sh_t[:], in1=sh_fix[:], op=ALU.add)
+        vec_b(0)
+        nc.vector.reciprocal(out=sh_inv[:], in_=sh_safe[:])
+        quantize("dx1")
+        product("tz2", "w2", "dx1", (0, 1,))
         vec_m(0)
         pool_d(0)
-        vec_n(1)
         vec_b(1)
-        quantize("dx1")
-        product("tz2", "w2", "dx1", (0,))
-        product("tz1", "w1", "dx1", (0,))
-        product("z1", "w1", "x1", (1,))
-        product("tz2", "w2", "dx1", (1,))
-        product("tz1", "w1", "dx1", (1,))
+        product("tz1", "w1", "dx1", (0, 1,))
         act_q(2)
+        act_q(3)
+        nc.scalar.activation(out=sh_half[:], in_=sh_safe[:], func=ACT.Copy, scale=0.5)
         act_t(2)
         act_z(2)
-        act_q(3)
         act_t(3)
         act_z(3)
+        vec_n(2)
         vec_m(1)
         pool_d(1)
-        vec_n(2)
+        vec_n(3)
         vec_a(2)
         vec_g(2)
         vec_b(2)
         vec_m(2)
         pool_d(2)
-        vec_n(3)
         vec_a(3)
+        vec_b(3)
         act_r1(0)
         act_r1(1)
         act_r1(2)
         act_r1(3)
         vec_f(0)
         vec_g(3)
-        vec_b(3)
         vec_f(1)
         vec_m(3)
         vec_f(2)

@@ -90,6 +90,9 @@ def tile_rows_pl_tnkernstudent_kernel(tc, x, w1, w2, sh, d0, dx, og, base, out_0
         def interleave(copy, dst, src):
             copy(out=dst.rearrange("p (c i) t -> p c t i", i=4), in_=src.rearrange("p t (c i) -> p c t i", i=4))
 
+        def interleave_plain(copy, dst, src):
+            copy(out=dst, in_=src.rearrange("p t c -> p c t"))
+
         def deal(copy, name):
             copy(
                 out=grp[name][:].rearrange("p (h c i) j -> p c j i h", h=H, i=2),
@@ -295,7 +298,7 @@ def tile_rows_pl_tnkernstudent_kernel(tc, x, w1, w2, sh, d0, dx, og, base, out_0
         vec_a(1)
         product("z2", "w2", "x1", (0, 1,))
         nc.scalar.activation(out=sh_sq[:], in_=sh_t[:], func=ACT.Square)
-        interleave(scopy, grp["dx1"][:], raw["dx1"][:])
+        interleave_plain(scopy, grp["dx1"][:], raw["dx1"][:])
         vec_g(0)
         vec_n(0)
         vec_g(1)
@@ -313,11 +316,11 @@ def tile_rows_pl_tnkernstudent_kernel(tc, x, w1, w2, sh, d0, dx, og, base, out_0
         product("tz1", "w1", "dx1", (0, 1,))
         act_q(2)
         act_q(3)
-        nc.scalar.activation(out=sh_half[:], in_=sh_safe[:], func=ACT.Copy, scale=0.5)
         act_t(2)
         act_z(2)
         act_t(3)
         act_z(3)
+        nc.scalar.activation(out=sh_half[:], in_=sh_safe[:], func=ACT.Copy, scale=0.5)
         vec_n(2)
         vec_m(1)
         pool_d(1)
@@ -341,11 +344,11 @@ def tile_rows_pl_tnkernstudent_kernel(tc, x, w1, w2, sh, d0, dx, og, base, out_0
         vec_d(3)
         vec_fh(3)
         vec_y(0)
-        interleave(scopy, y_grp[0][:], ty[0][:])
+        interleave_plain(scopy, y_grp[0][:], ty[0][:])
         vec_y(1)
         planes(0)
         interleave(vcopy, y_grp[1][:, :176, :], ty[1][:, :, :176])
-        interleave(scopy, y_grp[1][:, 176:, :], ty[1][:, :, 176:])
+        interleave_plain(scopy, y_grp[1][:, 176:, :], ty[1][:, :, 176:])
         planes(1)
         for quad in range(4):
             queue = nc.scalar if quad % 2 else nc.sync

@@ -16,11 +16,16 @@ ALU = mybir.AluOpType
 
 P = 128
 PACK = 4
-ROWS = 64
-H = 2
+ROWS = D // PACK
+H = M // P
 CHUNK = 256
-NCH = N // CHUNK
+CHUNKS = N // CHUNK
 MM_N = 128
+LINE = 4
+QUADRANT = 32
+SCALE_ROWS = 4
+SH_SQUARE_MIN = 2.0**-120
+SH_SHIFT = 2.0**-59
 
 
 def tile_rows_pl_tnkernstudent_kernel(tc, x, w1, w2, sh, d0, dx, og, base, out_0, out_1, out_2):
@@ -30,7 +35,7 @@ def tile_rows_pl_tnkernstudent_kernel(tc, x, w1, w2, sh, d0, dx, og, base, out_0
         ps = ctx.enter_context(tc.psum_pool(name="ps", bufs=1))
         ctx.enter_context(tc.manual_schedule())
 
-        def sbt(name, shape, dtype):
+        def sbuf(name, shape, dtype):
             return sb.tile(shape, dtype, name=name, align_bytes=64)
 
         def cols(c):
@@ -40,318 +45,289 @@ def tile_rows_pl_tnkernstudent_kernel(tc, x, w1, w2, sh, d0, dx, og, base, out_0
             return t[:, h * CHUNK : (h + 1) * CHUNK]
 
         def by_h(t):
-            return t[:].rearrange("p (h c) -> p h c", h=H)
+            return t[:].rearrange("q (h n) -> q h n", h=H)
 
-        raw, grp, codes, scales = {}, {}, {}, {}
-
-        def load_k(name, src):
-            raw[name] = sbt("raw_" + name, [P, PACK, CHUNK], F32)
-            grp[name] = sbt("grp_" + name, [P, CHUNK, PACK], BF16)
-            codes[name] = sbt("codes_" + name, [P, CHUNK], U32)
-            scales[name] = sbt("scales_" + name, [P, CHUNK], U8)
-            nc.sync.dma_start(out=raw[name][:], in_=src)
-
-        def k_first(t):
+        def four_rows(t):
             return t.rearrange("g (p j) n -> (g p) j n", j=PACK)
 
-        def load_rows(name, src):
-            t = sbt(name, [P, H, N], F32)
-            nc.sync.dma_start(out=t[:], in_=src.rearrange("(q h) n -> q h n", h=H))
+        raw, grouped, codes, scales = {}, {}, {}, {}
+
+        def load_operand(name, src):
+            raw[name] = sbuf("raw_" + name, [P, PACK, CHUNK], F32)
+            grouped[name] = sbuf("grouped_" + name, [P, CHUNK, PACK], BF16)
+            codes[name] = sbuf("codes_" + name, [P, CHUNK], U32)
+            scales[name] = sbuf("scales_" + name, [P, CHUNK], U8)
+            nc.sync.dma_start(out=raw[name][:], in_=src)
+
+        def load_d0(g):
+            t = sbuf("d0_%d" % g, [P, H, N], F32)
+            nc.sync.dma_start(out=t[:], in_=d0[g].rearrange("(q h) n -> q h n", h=H))
             return t
 
-        def load_feature(name, src):
-            t = sbt(name, [P, G, H], F32)
-            nc.scalar.dma_start(out=t[:], in_=src.rearrange("g (q h) o -> q g (h o)", h=H))
-            return t
+        sh_sb = sbuf("sh_sb", [P, G, H], F32)
+        og_sb = sbuf("og_sb", [P, PACK], F32)
+        base_sb = sbuf("base_sb", [P, PACK, N], F32)
+        load_operand("w2", four_rows(w2))
+        load_operand("x0", four_rows(x)[:, :, cols(0)])
+        load_operand("dx0", four_rows(dx)[:, :, cols(0)])
+        load_operand("w1", four_rows(w1))
+        load_operand("x1", four_rows(x)[:, :, cols(1)])
+        d0_sb = [load_d0(0)]
+        nc.sync.dma_start(out=sh_sb[:], in_=sh.rearrange("g (q h) o -> q g (h o)", h=H))
+        load_operand("dx1", four_rows(dx)[:, :, cols(1)])
+        d0_sb.append(load_d0(1))
+        nc.sync.dma_start(out=og_sb[:], in_=og.rearrange("g (s u) o -> (g s) (u o)", u=PACK))
+        nc.sync.dma_start(out=base_sb[:], in_=four_rows(base))
 
-        sh_t = sbt("sh_t", [P, G, H], F32)
-        og_t = sbt("og_t", [P, PACK], F32)
-        load_k("w2", k_first(w2))
-        load_k("x0", k_first(x)[:, :, cols(0)])
-        load_k("dx0", k_first(dx)[:, :, cols(0)])
-        load_k("w1", k_first(w1))
-        d0_t = {}
+        def interleave(dst, src):
+            nc.vector.tensor_copy(
+                out=dst.rearrange("p (c i) j -> p c j i", i=LINE), in_=src.rearrange("p j (c i) -> p c j i", i=LINE)
+            )
 
-        def load_d0(g, c):
-            d0_t[g, c] = sbt("d0_%d_%d" % (g, c), [P, H, CHUNK], F32)
-            nc.sync.dma_start(out=d0_t[g, c][:], in_=d0[g].rearrange("(q h) n -> q h n", h=H)[:, :, cols(c)])
+        def round_inputs(name):
+            interleave(grouped[name][:], raw[name][:])
 
-        load_k("x1", k_first(x)[:, :, cols(1)])
-        load_d0(0, 0)
-        load_d0(1, 0)
-        nc.sync.dma_start(out=sh_t[:], in_=sh.rearrange("g (q h) o -> q g (h o)", h=H))
-        load_k("dx1", k_first(dx)[:, :, cols(1)])
-        load_d0(0, 1)
-        load_d0(1, 1)
-        nc.sync.dma_start(out=og_t[:], in_=og.rearrange("g (s u) o -> (g s) (u o)", u=PACK))
-        base_t = sbt("base_t", [P, PACK, N], F32)
-        nc.sync.dma_start(out=base_t[:], in_=k_first(base))
-
-        def interleave(copy, dst, src):
-            copy(out=dst.rearrange("p (c i) t -> p c t i", i=4), in_=src.rearrange("p t (c i) -> p c t i", i=4))
-
-        def interleave_plain(copy, dst, src):
-            copy(out=dst, in_=src.rearrange("p t c -> p c t"))
-
-        def deal(copy, name):
-            copy(
-                out=grp[name][:].rearrange("p (h c i) j -> p c j i h", h=H, i=2),
-                in_=raw[name][:].rearrange("p j (c i h) -> p c j i h", h=H, i=2),
+        def round_weights(name):
+            nc.vector.tensor_copy(
+                out=grouped[name][:].rearrange("p (h c i) j -> p c j i h", h=H, i=LINE // H),
+                in_=raw[name][:].rearrange("p j (c i h) -> p c j i h", h=H, i=LINE // H),
             )
 
         def quantize(name):
             nc.vector.quantize_mx(
-                out=codes[name][:].bitcast(FP8X4), scales=scales[name][:], in_=grp[name][:].rearrange("p c t -> p (c t)")
+                out=codes[name][:].bitcast(FP8X4),
+                scales=scales[name][:],
+                in_=grouped[name][:].rearrange("p n j -> p (n j)"),
             )
 
-        bank = {}
-        for prod in ("z2", "tz2", "z1", "tz1"):
-            for g in range(G):
-                bank[prod, g] = ps.tile([P, H * CHUNK], F32, name="ps_%s_%d" % (prod, g))
+        banks = [[ps.tile([P, H * CHUNK], F32, name="bank_%d_%d" % (g, i)) for i in range(4)] for g in range(G)]
 
-        def product(prod, w, a, groups):
+        def bank(product, g, c):
+            return banks[g][{"z2": c, "tz2": 1 - c, "z1": 2, "tz1": 3}[product]]
+
+        def multiply(product, c):
+            w = "w" + product[-1]
+            a = ("dx%d" if product.startswith("t") else "x%d") % c
             for h in range(H):
                 for n0 in range(0, CHUNK, MM_N):
-                    for g in groups:
+                    for g in range(G):
                         rows = slice(g * ROWS, (g + 1) * ROWS)
-                        wc = slice(h * P, (h + 1) * P)
-                        ac = slice(n0, n0 + MM_N)
+                        w_cols = slice(h * P, (h + 1) * P)
+                        a_cols = slice(n0, n0 + MM_N)
                         nc.tensor.matmul_mx(
-                            out=bank[prod, g][:, h * CHUNK + n0 : h * CHUNK + n0 + MM_N],
-                            lhsT=codes[w][rows, wc].bitcast(FP8X4),
-                            lhsT_scale=scales[w][rows, wc],
-                            rhs=codes[a][rows, ac].bitcast(FP8X4),
-                            rhs_scale=scales[a][rows, ac],
+                            out=half(bank(product, g, c), h)[:, a_cols],
+                            lhsT=codes[w][rows, w_cols].bitcast(FP8X4),
+                            lhsT_scale=scales[w][rows, w_cols],
+                            rhs=codes[a][rows, a_cols].bitcast(FP8X4),
+                            rhs_scale=scales[a][rows, a_cols],
                             start=True,
                             stop=True,
                         )
 
-        units = [(g, c) for c in range(NCH) for g in range(G)]
-        tq, tt, tz, ta, tn, tb, tr = [], [], [], [], [], [], []
-        for u in range(len(units)):
-            for lst, nm in ((tq, "q"), (tt, "t"), (tz, "z"), (ta, "a"), (tn, "n"), (tb, "b"), (tr, "r")):
-                lst.append(sbt("%s_%d" % (nm, u), [P, H * CHUNK], F32))
+        units = [(g, c) for c in range(CHUNKS) for g in range(G)]
 
-        one = sbt("one", [P, 1], F32)
-        sh_sq = sbt("sh_sq", [P, G, H], F32)
-        sh_fix = sbt("sh_fix", [P, G, H], F32)
-        sh_safe = sbt("sh_safe", [P, G, H], F32)
-        sh_inv = sbt("sh_inv", [P, G, H], F32)
-        sh_half = sbt("sh_half", [P, G, H], F32)
+        def unit_tiles(name):
+            return [sbuf("%s_%d" % (name, i), [P, H * CHUNK], F32) for i in range(len(units))]
+
+        silu_neg = unit_tiles("silu_neg")
+        z2_sb = unit_tiles("z2_sb")
+        tanh_half = unit_tiles("tanh_half")
+        dist = unit_tiles("dist")
+        slope = unit_tiles("slope")
+        change = unit_tiles("change")
+        inv_sq = unit_tiles("inv_sq")
+
+        one = sbuf("one", [P, 1], F32)
+        sh_sq = sbuf("sh_sq", [P, G, H], F32)
+        sh_shift = sbuf("sh_shift", [P, G, H], F32)
+        sh_safe = sbuf("sh_safe", [P, G, H], F32)
+        sh_inv = sbuf("sh_inv", [P, G, H], F32)
+        sh_half = sbuf("sh_half", [P, G, H], F32)
         nc.gpsimd.memset(one[:], 1.0)
 
-        def act_q(u):
-            nc.scalar.activation(out=tq[u][:], in_=bank["z2", units[u][0]][:], func=ACT.Silu, scale=-1.0)
+        def read_z2(c):
+            pair = [i for i in range(len(units)) if units[i][1] == c]
+            for i in pair:
+                nc.scalar.activation(out=silu_neg[i][:], in_=bank("z2", *units[i])[:], func=ACT.Silu, scale=-1.0)
+            for i in pair:
+                nc.scalar.copy(out=z2_sb[i][:], in_=bank("z2", *units[i])[:])
+            for i in pair:
+                nc.scalar.activation(out=tanh_half[i][:], in_=bank("z2", *units[i])[:], func=ACT.Tanh, scale=0.5)
 
-        def act_z(u):
-            nc.scalar.activation(out=tz[u][:], in_=bank["z2", units[u][0]][:], func=ACT.Silu)
-
-        def act_t(u):
-            nc.scalar.activation(out=tt[u][:], in_=bank["z2", units[u][0]][:], func=ACT.Tanh, scale=0.5)
-
-        def vec_a(u):
-            nc.vector.scalar_tensor_tensor(
-                out=ta[u][:], in0=tq[u][:], scalar=1.0, in1=bank["tz2", units[u][0]][:], op0=ALU.subtract, op1=ALU.mult
-            )
-
-        def vec_n(u):
-            g, c = units[u]
-            nc.vector.tensor_tensor(out=by_h(tn[u]), in0=d0_t[g, c][:], in1=by_h(bank["z1", g]), op=ALU.subtract)
-
-        def vec_b(u):
-            nc.vector.scalar_tensor_tensor(
-                out=tb[u][:], in0=bank["tz1", units[u][0]][:], scalar=2.0, in1=tz[u][:], op0=ALU.mult, op1=ALU.mult
-            )
-
-        def vec_g(u):
-            nc.vector.scalar_tensor_tensor(
-                out=ta[u][:], in0=tt[u][:], scalar=1.0, in1=ta[u][:], op0=ALU.add, op1=ALU.mult
-            )
-
-        def vec_m(u):
-            g = units[u][0]
-            for h in range(H):
-                nc.vector.scalar_tensor_tensor(
-                    out=half(ta[u], h), in0=half(tn[u], h), scalar=sh_inv[:, g, h : h + 1], in1=half(ta[u], h),
-                    op0=ALU.add, op1=ALU.mult,
-                )
-
-        def pool_d(u):
-            nc.gpsimd.tensor_tensor(out=tb[u][:], in0=tb[u][:], in1=ta[u][:], op=ALU.subtract)
-
-        def vec_d(u):
-            nc.vector.tensor_tensor(out=tb[u][:], in0=tb[u][:], in1=ta[u][:], op=ALU.subtract)
-
-        vcopy, scopy = nc.vector.tensor_copy, nc.scalar.copy
-
-        def gcopy(out, in_):
-            nc.gpsimd.tensor_scalar(out=out, in0=in_, scalar1=1.0, scalar2=0.0, op0=ALU.mult, op1=ALU.add)
-
-        gathered = [sbt("gathered_%d" % c, [P, PACK, CHUNK], F32) for c in range(NCH)]
-        out_rows = out_0.rearrange("(p u) n -> p u n", u=PACK)
-        ty = [sbt("y_%d" % c, [P, PACK, CHUNK], F32) for c in range(NCH)]
-        y_scales = sbt("y_scales", [P, N], U8)
-        words = out_1[0].rearrange("p n u -> p (n u)").bitcast(I32)
-        y_grp = [sbt("y_grp_%d" % c, [P, CHUNK, PACK], BF16) for c in range(NCH)]
-        y_codes = [sbt("y_codes_%d" % c, [P, CHUNK], U32) for c in range(NCH)]
-
-        def act_r(pair):
-            for u in pair:
-                g = units[u][0]
-                for h in range(H):
-                    nc.scalar.activation(
-                        out=half(tr[u], h), in_=half(tn[u], h), func=ACT.Abs_reciprocal_sqrt,
-                        scale=sh_t[:, g, h : h + 1], bias=one[:],
-                    )
-            for rep in range(2):
-                for u in pair:
-                    nc.scalar.activation(out=tr[u][:], in_=tr[u][:], func=ACT.Square)
-
-        def act_r1(u):
-            g = units[u][0]
+        def inverse_square(i):
+            g = units[i][0]
             for h in range(H):
                 nc.scalar.activation(
-                    out=half(tr[u], h), in_=half(tn[u], h), func=ACT.Abs_reciprocal_sqrt,
-                    scale=sh_t[:, g, h : h + 1], bias=one[:],
+                    out=half(inv_sq[i], h),
+                    in_=half(dist[i], h),
+                    func=ACT.Abs_reciprocal_sqrt,
+                    scale=sh_sb[:, g, h : h + 1],
+                    bias=one[:],
                 )
-            for rep in range(2):
+            for squaring in range(2):
                 for h in range(H):
-                    nc.scalar.activation(out=half(tr[u], h), in_=half(tr[u], h), func=ACT.Square)
+                    nc.scalar.activation(out=half(inv_sq[i], h), in_=half(inv_sq[i], h), func=ACT.Square)
 
-        def pool_f(u):
-            nc.gpsimd.tensor_tensor(out=tb[u][:], in0=tb[u][:], in1=tr[u][:], op=ALU.mult)
-
-        def f_half(u, h):
+        def read_tz2(i):
             nc.vector.scalar_tensor_tensor(
-                out=half(tb[u], h), in0=half(tb[u], h), scalar=sh_half[:, units[u][0], h : h + 1], in1=half(tr[u], h),
-                op0=ALU.mult, op1=ALU.mult,
+                out=slope[i][:],
+                in0=silu_neg[i][:],
+                scalar=1.0,
+                in1=bank("tz2", *units[i])[:],
+                op0=ALU.subtract,
+                op1=ALU.mult,
             )
 
-        def vec_f(u):
+        def read_z1(i):
+            g, c = units[i]
+            nc.vector.tensor_tensor(
+                out=by_h(dist[i]), in0=d0_sb[g][:, :, cols(c)], in1=by_h(bank("z1", g, c)), op=ALU.subtract
+            )
+
+        def read_tz1(i):
+            nc.vector.tensor_tensor(out=change[i][:], in0=z2_sb[i][:], in1=bank("tz1", *units[i])[:], op=ALU.mult)
+
+        def slope_times_den(i):
+            g = units[i][0]
             for h in range(H):
-                f_half(u, h)
-            gather(u, (0, 1))
+                nc.vector.scalar_tensor_tensor(
+                    out=half(slope[i], h),
+                    in0=half(dist[i], h),
+                    scalar=sh_inv[:, g, h : h + 1],
+                    in1=half(slope[i], h),
+                    op0=ALU.add,
+                    op1=ALU.mult,
+                )
 
-        def gather(u, hs):
-            g, c = units[u]
-            dst = gathered[c][g * ROWS : (g + 1) * ROWS].rearrange("s (b h) c -> s b h c", h=H)
-            if len(hs) == H:
-                nc.sync.dma_start(out=dst.rearrange("s b h c -> s b (h c)"), in_=tb[u][:])
-            else:
-                nc.sync.dma_start(out=dst[:, :, hs[0], :], in_=half(tb[u], hs[0]))
+        def subtract_slope(engine, i):
+            engine.tensor_tensor(out=change[i][:], in0=change[i][:], in1=slope[i][:], op=ALU.subtract)
 
-        def vec_fh(u):
+        def times_sigmoid(i):
+            nc.vector.scalar_tensor_tensor(
+                out=change[i][:], in0=tanh_half[i][:], scalar=1.0, in1=change[i][:], op0=ALU.add, op1=ALU.mult
+            )
+
+        xh_rows = [sbuf("xh_rows_%d" % c, [P, PACK, CHUNK], F32) for c in range(CHUNKS)]
+
+        def finish_xh(i, dma_per_half):
+            g, c = units[i]
+            dst = xh_rows[c][g * ROWS : (g + 1) * ROWS].rearrange("s (b h) n -> s b h n", h=H)
             for h in range(H):
-                f_half(u, h)
-                gather(u, (h,))
-
-        def vec_y(c):
-            for u in (0, 2, 1, 3):
                 nc.vector.scalar_tensor_tensor(
-                    out=ty[c][:, u, :], in0=gathered[c][:, u, :], scalar=og_t[:, u : u + 1], in1=base_t[:, u, cols(c)],
-                    op0=ALU.mult, op1=ALU.add,
+                    out=half(change[i], h),
+                    in0=half(change[i], h),
+                    scalar=sh_half[:, g, h : h + 1],
+                    in1=half(inv_sq[i], h),
+                    op0=ALU.mult,
+                    op1=ALU.mult,
                 )
-                if u >= 2:
-                    nc.sync.dma_start(out=out_rows[:, u - 2 :: 2, cols(c)], in_=ty[c][:, u - 2 :: 2, :])
+                if dma_per_half:
+                    nc.sync.dma_start(out=dst[:, :, h, :], in_=half(change[i], h))
+            if not dma_per_half:
+                nc.sync.dma_start(out=dst.rearrange("s b h n -> s b (h n)"), in_=change[i][:])
 
-        def vec_y_cols(c, lo, hi):
-            for u in range(PACK):
-                nc.vector.scalar_tensor_tensor(
-                    out=ty[c][:, u, lo:hi], in0=gathered[c][:, u, lo:hi], scalar=og_t[:, u : u + 1],
-                    in1=base_t[:, u, c * CHUNK + lo : c * CHUNK + hi], op0=ALU.mult, op1=ALU.add,
-                )
-            nc.sync.dma_start(out=out_rows[:, :, c * CHUNK + lo : c * CHUNK + hi], in_=ty[c][:, :, lo:hi])
-
-        def planes_cols(c, lo, hi):
-            nc.vector.quantize_mx(
-                out=y_codes[c][:, lo:hi].bitcast(FP8X4), scales=y_scales[:, c * CHUNK + lo : c * CHUNK + hi],
-                in_=y_grp[c][:, lo:hi, :].rearrange("p c t -> p (c t)"),
-            )
-
-        def planes(c):
-            nc.vector.quantize_mx(
-                out=y_codes[c][:].bitcast(FP8X4), scales=y_scales[:, cols(c)], in_=y_grp[c][:].rearrange("p c t -> p (c t)")
-            )
-            nc.sync.dma_start(out=words[:, cols(c)], in_=y_codes[c][:].bitcast(I32))
-
-        deal(vcopy, "w2")
+        round_weights("w2")
         quantize("w2")
-        interleave(vcopy, grp["x0"][:], raw["x0"][:])
+        round_inputs("x0")
         quantize("x0")
-        product("z2", "w2", "x0", (0, 1,))
-        interleave(vcopy, grp["dx0"][:], raw["dx0"][:])
+        multiply("z2", 0)
+        round_inputs("dx0")
         quantize("dx0")
-        product("tz2", "w2", "dx0", (0, 1,))
-        deal(vcopy, "w1")
+        multiply("tz2", 0)
+        round_weights("w1")
         quantize("w1")
-        product("z1", "w1", "x0", (0, 1,))
-        product("tz1", "w1", "dx0", (0, 1,))
-        act_q(0)
-        act_q(1)
-        act_t(0)
-        act_t(1)
-        act_z(0)
-        act_z(1)
-        interleave(vcopy, grp["x1"][:], raw["x1"][:])
-        vec_a(0)
+        multiply("z1", 0)
+        multiply("tz1", 0)
+        read_z2(0)
+
+        round_inputs("x1")
+        read_tz2(0)
         quantize("x1")
-        vec_a(1)
-        product("z2", "w2", "x1", (0, 1,))
-        nc.scalar.activation(out=sh_sq[:], in_=sh_t[:], func=ACT.Square)
-        interleave_plain(scopy, grp["dx1"][:], raw["dx1"][:])
-        vec_g(0)
-        vec_n(0)
-        vec_g(1)
-        nc.vector.tensor_scalar(out=sh_fix[:], in0=sh_sq[:], scalar1=2.0**-120, scalar2=2.0**-59, op0=ALU.is_lt, op1=ALU.mult)
-        vec_n(1)
-        product("z1", "w1", "x1", (0, 1,))
-        nc.vector.tensor_tensor(out=sh_safe[:], in0=sh_t[:], in1=sh_fix[:], op=ALU.add)
-        vec_b(0)
+        read_tz2(1)
+        multiply("z2", 1)
+        read_z2(1)
+        nc.vector.tensor_tensor(out=sh_sq[:], in0=sh_sb[:], in1=sh_sb[:], op=ALU.mult)
+        read_z1(0)
+        nc.vector.tensor_scalar(
+            out=sh_shift[:], in0=sh_sq[:], scalar1=SH_SQUARE_MIN, scalar2=SH_SHIFT, op0=ALU.is_lt, op1=ALU.mult
+        )
+        read_tz1(0)
+        nc.vector.tensor_tensor(out=sh_safe[:], in0=sh_sb[:], in1=sh_shift[:], op=ALU.add)
+        round_inputs("dx1")
         nc.vector.reciprocal(out=sh_inv[:], in_=sh_safe[:])
+        read_z1(1)
+        multiply("z1", 1)
         quantize("dx1")
-        product("tz2", "w2", "dx1", (0, 1,))
-        vec_m(0)
-        pool_d(0)
-        vec_b(1)
-        product("tz1", "w1", "dx1", (0, 1,))
-        act_q(2)
-        act_q(3)
-        act_t(2)
-        act_z(2)
-        act_t(3)
-        act_z(3)
-        nc.scalar.activation(out=sh_half[:], in_=sh_safe[:], func=ACT.Copy, scale=0.5)
-        vec_n(2)
-        vec_m(1)
-        pool_d(1)
-        vec_n(3)
-        vec_a(2)
-        vec_g(2)
-        vec_b(2)
-        vec_m(2)
-        pool_d(2)
-        vec_a(3)
-        vec_b(3)
-        act_r1(0)
-        act_r1(1)
-        act_r1(2)
-        act_r1(3)
-        vec_f(0)
-        vec_g(3)
-        vec_f(1)
-        vec_m(3)
-        vec_f(2)
-        vec_d(3)
-        vec_fh(3)
-        vec_y(0)
-        interleave_plain(scopy, y_grp[0][:], ty[0][:])
-        vec_y(1)
-        planes(0)
-        interleave(vcopy, y_grp[1][:, :176, :], ty[1][:, :, :176])
-        interleave_plain(scopy, y_grp[1][:, 176:, :], ty[1][:, :, 176:])
-        planes(1)
-        for quad in range(4):
+        multiply("tz2", 1)
+
+        slope_times_den(0)
+        subtract_slope(nc.gpsimd, 0)
+        read_tz1(1)
+        multiply("tz1", 1)
+        read_z1(2)
+        nc.vector.tensor_scalar(out=sh_half[:], in0=sh_safe[:], scalar1=0.5, scalar2=None, op0=ALU.mult)
+        slope_times_den(1)
+        subtract_slope(nc.gpsimd, 1)
+        read_z1(3)
+        read_tz2(2)
+        read_tz1(2)
+        times_sigmoid(0)
+        slope_times_den(2)
+        subtract_slope(nc.gpsimd, 2)
+        read_tz2(3)
+        read_tz1(3)
+
+        for i in range(len(units)):
+            inverse_square(i)
+
+        finish_xh(0, False)
+        times_sigmoid(1)
+        slope_times_den(3)
+        finish_xh(1, False)
+        times_sigmoid(2)
+        subtract_slope(nc.vector, 3)
+        finish_xh(2, False)
+        times_sigmoid(3)
+        finish_xh(3, True)
+
+        out_rows = out_0.rearrange("(r u) n -> r u n", u=PACK)
+        out_words = out_1[0].rearrange("r n u -> r (n u)").bitcast(I32)
+        y_scales = sbuf("y_scales", [P, N], U8)
+        y = [sbuf("y_%d" % c, [P, PACK, CHUNK], F32) for c in range(CHUNKS)]
+        y_grouped = [sbuf("y_grouped_%d" % c, [P, CHUNK, PACK], BF16) for c in range(CHUNKS)]
+        y_codes = [sbuf("y_codes_%d" % c, [P, CHUNK], U32) for c in range(CHUNKS)]
+
+        def finish_y(c):
+            for h in range(H):
+                for u in range(h, PACK, H):
+                    nc.vector.scalar_tensor_tensor(
+                        out=y[c][:, u, :],
+                        in0=xh_rows[c][:, u, :],
+                        scalar=og_sb[:, u : u + 1],
+                        in1=base_sb[:, u, cols(c)],
+                        op0=ALU.mult,
+                        op1=ALU.add,
+                    )
+                nc.sync.dma_start(out=out_rows[:, h::H, cols(c)], in_=y[c][:, h::H, :])
+
+        def quantize_y(c):
+            nc.vector.quantize_mx(
+                out=y_codes[c][:].bitcast(FP8X4),
+                scales=y_scales[:, cols(c)],
+                in_=y_grouped[c][:].rearrange("r n u -> r (n u)"),
+            )
+            nc.sync.dma_start(out=out_words[:, cols(c)], in_=y_codes[c][:].bitcast(I32))
+
+        finish_y(0)
+        interleave(y_grouped[0][:], y[0][:])
+        finish_y(1)
+        quantize_y(0)
+        interleave(y_grouped[1][:], y[1][:])
+        quantize_y(1)
+
+        for quad in range(P // QUADRANT):
             queue = nc.scalar if quad % 2 else nc.sync
             queue.dma_start(
-                out=out_2[0, 4 * quad : 4 * quad + 4, :].bitcast(I32), in_=y_scales[32 * quad : 32 * quad + 4, :].bitcast(I32)
+                out=out_2[0, SCALE_ROWS * quad : SCALE_ROWS * (quad + 1), :].bitcast(I32),
+                in_=y_scales[QUADRANT * quad : QUADRANT * quad + SCALE_ROWS, :].bitcast(I32),
             )

from contextlib import ExitStack

import concourse.mybir as mybir

G, D, M, N = 2, 256, 256, 512
FLOPS = 4 * 2 * G * D * M * N

F32 = mybir.dt.float32
BF16 = mybir.dt.bfloat16
U32 = mybir.dt.uint32
I32 = mybir.dt.int32
U8 = mybir.dt.uint8
FP8X4 = mybir.dt.float8_e4m3fn_x4
ACT = mybir.ActivationFunctionType
ALU = mybir.AluOpType

P = 128
PACK = 4
ROWS = D // PACK
H = M // P
CHUNK = 256
CHUNKS = N // CHUNK
MM_N = 128
LINE = 4
QUADRANT = 32
SCALE_ROWS = 4
SH_SQUARE_MIN = 2.0**-120
SH_SHIFT = 2.0**-59


def tile_rows_pl_tnkernstudent_kernel(tc, x, w1, w2, sh, d0, dx, og, base, out_0, out_1, out_2):
    nc = tc.nc
    with ExitStack() as ctx:
        sb = ctx.enter_context(tc.tile_pool(name="sb", bufs=1))
        ps = ctx.enter_context(tc.psum_pool(name="ps", bufs=1))
        ctx.enter_context(tc.manual_schedule())

        def sbuf(name, shape, dtype):
            return sb.tile(shape, dtype, name=name, align_bytes=64)

        def cols(c):
            return slice(c * CHUNK, (c + 1) * CHUNK)

        def half(t, h):
            return t[:, h * CHUNK : (h + 1) * CHUNK]

        def by_h(t):
            return t[:].rearrange("q (h n) -> q h n", h=H)

        def four_rows(t):
            return t.rearrange("g (p j) n -> (g p) j n", j=PACK)

        raw, grouped, codes, scales = {}, {}, {}, {}

        def load_operand(name, src):
            raw[name] = sbuf("raw_" + name, [P, PACK, CHUNK], F32)
            grouped[name] = sbuf("grouped_" + name, [P, CHUNK, PACK], BF16)
            codes[name] = sbuf("codes_" + name, [P, CHUNK], U32)
            scales[name] = sbuf("scales_" + name, [P, CHUNK], U8)
            nc.sync.dma_start(out=raw[name][:], in_=src)

        def load_d0(g):
            t = sbuf("d0_%d" % g, [P, H, N], F32)
            nc.sync.dma_start(out=t[:], in_=d0[g].rearrange("(q h) n -> q h n", h=H))
            return t

        sh_sb = sbuf("sh_sb", [P, G, H], F32)
        og_sb = sbuf("og_sb", [P, PACK], F32)
        base_sb = sbuf("base_sb", [P, PACK, N], F32)
        load_operand("w2", four_rows(w2))
        load_operand("x0", four_rows(x)[:, :, cols(0)])
        load_operand("dx0", four_rows(dx)[:, :, cols(0)])
        load_operand("w1", four_rows(w1))
        load_operand("x1", four_rows(x)[:, :, cols(1)])
        d0_sb = [load_d0(0)]
        nc.sync.dma_start(out=sh_sb[:], in_=sh.rearrange("g (q h) o -> q g (h o)", h=H))
        load_operand("dx1", four_rows(dx)[:, :, cols(1)])
        d0_sb.append(load_d0(1))
        nc.sync.dma_start(out=og_sb[:], in_=og.rearrange("g (s u) o -> (g s) (u o)", u=PACK))
        nc.sync.dma_start(out=base_sb[:], in_=four_rows(base))

        def interleave(dst, src):
            nc.vector.tensor_copy(
                out=dst.rearrange("p (c i) j -> p c j i", i=LINE), in_=src.rearrange("p j (c i) -> p c j i", i=LINE)
            )

        def round_inputs(name):
            interleave(grouped[name][:], raw[name][:])

        def round_weights(name):
            nc.vector.tensor_copy(
                out=grouped[name][:].rearrange("p (h c i) j -> p c j i h", h=H, i=LINE // H),
                in_=raw[name][:].rearrange("p j (c i h) -> p c j i h", h=H, i=LINE // H),
            )

        def quantize(name):
            nc.vector.quantize_mx(
                out=codes[name][:].bitcast(FP8X4),
                scales=scales[name][:],
                in_=grouped[name][:].rearrange("p n j -> p (n j)"),
            )

        banks = [[ps.tile([P, H * CHUNK], F32, name="bank_%d_%d" % (g, i)) for i in range(4)] for g in range(G)]

        def bank(product, g, c):
            return banks[g][{"z2": c, "tz2": 1 - c, "z1": 2, "tz1": 3}[product]]

        def multiply(product, c):
            w = "w" + product[-1]
            a = ("dx%d" if product.startswith("t") else "x%d") % c
            for h in range(H):
                for n0 in range(0, CHUNK, MM_N):
                    for g in range(G):
                        rows = slice(g * ROWS, (g + 1) * ROWS)
                        w_cols = slice(h * P, (h + 1) * P)
                        a_cols = slice(n0, n0 + MM_N)
                        nc.tensor.matmul_mx(
                            out=half(bank(product, g, c), h)[:, a_cols],
                            lhsT=codes[w][rows, w_cols].bitcast(FP8X4),
                            lhsT_scale=scales[w][rows, w_cols],
                            rhs=codes[a][rows, a_cols].bitcast(FP8X4),
                            rhs_scale=scales[a][rows, a_cols],
                            start=True,
                            stop=True,
                        )

        units = [(g, c) for c in range(CHUNKS) for g in range(G)]

        def unit_tiles(name):
            return [sbuf("%s_%d" % (name, i), [P, H * CHUNK], F32) for i in range(len(units))]

        silu_neg = unit_tiles("silu_neg")
        z2_sb = unit_tiles("z2_sb")
        tanh_half = unit_tiles("tanh_half")
        dist = unit_tiles("dist")
        slope = unit_tiles("slope")
        change = unit_tiles("change")
        inv_sq = unit_tiles("inv_sq")

        one = sbuf("one", [P, 1], F32)
        sh_sq = sbuf("sh_sq", [P, G, H], F32)
        sh_shift = sbuf("sh_shift", [P, G, H], F32)
        sh_safe = sbuf("sh_safe", [P, G, H], F32)
        sh_inv = sbuf("sh_inv", [P, G, H], F32)
        sh_half = sbuf("sh_half", [P, G, H], F32)
        nc.gpsimd.memset(one[:], 1.0)

        def read_z2(c):
            pair = [i for i in range(len(units)) if units[i][1] == c]
            for i in pair:
                nc.scalar.activation(out=silu_neg[i][:], in_=bank("z2", *units[i])[:], func=ACT.Silu, scale=-1.0)
            for i in pair:
                nc.scalar.copy(out=z2_sb[i][:], in_=bank("z2", *units[i])[:])
            for i in pair:
                nc.scalar.activation(out=tanh_half[i][:], in_=bank("z2", *units[i])[:], func=ACT.Tanh, scale=0.5)

        def inverse_square(i):
            g = units[i][0]
            for h in range(H):
                nc.scalar.activation(
                    out=half(inv_sq[i], h),
                    in_=half(dist[i], h),
                    func=ACT.Abs_reciprocal_sqrt,
                    scale=sh_sb[:, g, h : h + 1],
                    bias=one[:],
                )
            for squaring in range(2):
                for h in range(H):
                    nc.scalar.activation(out=half(inv_sq[i], h), in_=half(inv_sq[i], h), func=ACT.Square)

        def read_tz2(i):
            nc.vector.scalar_tensor_tensor(
                out=slope[i][:],
                in0=silu_neg[i][:],
                scalar=1.0,
                in1=bank("tz2", *units[i])[:],
                op0=ALU.subtract,
                op1=ALU.mult,
            )

        def read_z1(i):
            g, c = units[i]
            nc.vector.tensor_tensor(
                out=by_h(dist[i]), in0=d0_sb[g][:, :, cols(c)], in1=by_h(bank("z1", g, c)), op=ALU.subtract
            )

        def read_tz1(i):
            nc.vector.tensor_tensor(out=change[i][:], in0=z2_sb[i][:], in1=bank("tz1", *units[i])[:], op=ALU.mult)

        def slope_times_den(i):
            g = units[i][0]
            for h in range(H):
                nc.vector.scalar_tensor_tensor(
                    out=half(slope[i], h),
                    in0=half(dist[i], h),
                    scalar=sh_inv[:, g, h : h + 1],
                    in1=half(slope[i], h),
                    op0=ALU.add,
                    op1=ALU.mult,
                )

        def subtract_slope(engine, i):
            engine.tensor_tensor(out=change[i][:], in0=change[i][:], in1=slope[i][:], op=ALU.subtract)

        def times_sigmoid(i):
            nc.vector.scalar_tensor_tensor(
                out=change[i][:], in0=tanh_half[i][:], scalar=1.0, in1=change[i][:], op0=ALU.add, op1=ALU.mult
            )

        xh_rows = [sbuf("xh_rows_%d" % c, [P, PACK, CHUNK], F32) for c in range(CHUNKS)]

        def finish_xh(i, dma_per_half):
            g, c = units[i]
            dst = xh_rows[c][g * ROWS : (g + 1) * ROWS].rearrange("s (b h) n -> s b h n", h=H)
            for h in range(H):
                nc.vector.scalar_tensor_tensor(
                    out=half(change[i], h),
                    in0=half(change[i], h),
                    scalar=sh_half[:, g, h : h + 1],
                    in1=half(inv_sq[i], h),
                    op0=ALU.mult,
                    op1=ALU.mult,
                )
                if dma_per_half:
                    nc.sync.dma_start(out=dst[:, :, h, :], in_=half(change[i], h))
            if not dma_per_half:
                nc.sync.dma_start(out=dst.rearrange("s b h n -> s b (h n)"), in_=change[i][:])

        round_weights("w2")
        quantize("w2")
        round_inputs("x0")
        quantize("x0")
        multiply("z2", 0)
        round_inputs("dx0")
        quantize("dx0")
        multiply("tz2", 0)
        round_weights("w1")
        quantize("w1")
        multiply("z1", 0)
        multiply("tz1", 0)
        read_z2(0)

        round_inputs("x1")
        read_tz2(0)
        quantize("x1")
        read_tz2(1)
        multiply("z2", 1)
        read_z2(1)
        nc.vector.tensor_tensor(out=sh_sq[:], in0=sh_sb[:], in1=sh_sb[:], op=ALU.mult)
        read_z1(0)
        nc.vector.tensor_scalar(
            out=sh_shift[:], in0=sh_sq[:], scalar1=SH_SQUARE_MIN, scalar2=SH_SHIFT, op0=ALU.is_lt, op1=ALU.mult
        )
        read_tz1(0)
        nc.vector.tensor_tensor(out=sh_safe[:], in0=sh_sb[:], in1=sh_shift[:], op=ALU.add)
        round_inputs("dx1")
        nc.vector.reciprocal(out=sh_inv[:], in_=sh_safe[:])
        read_z1(1)
        multiply("z1", 1)
        quantize("dx1")
        multiply("tz2", 1)

        slope_times_den(0)
        subtract_slope(nc.gpsimd, 0)
        read_tz1(1)
        multiply("tz1", 1)
        read_z1(2)
        nc.vector.tensor_scalar(out=sh_half[:], in0=sh_safe[:], scalar1=0.5, scalar2=None, op0=ALU.mult)
        slope_times_den(1)
        subtract_slope(nc.gpsimd, 1)
        read_z1(3)
        read_tz2(2)
        read_tz1(2)
        times_sigmoid(0)
        slope_times_den(2)
        subtract_slope(nc.gpsimd, 2)
        read_tz2(3)
        read_tz1(3)

        for i in range(len(units)):
            inverse_square(i)

        finish_xh(0, False)
        times_sigmoid(1)
        slope_times_den(3)
        finish_xh(1, False)
        times_sigmoid(2)
        subtract_slope(nc.vector, 3)
        finish_xh(2, False)
        times_sigmoid(3)
        finish_xh(3, True)

        out_rows = out_0.rearrange("(r u) n -> r u n", u=PACK)
        out_words = out_1[0].rearrange("r n u -> r (n u)").bitcast(I32)
        y_scales = sbuf("y_scales", [P, N], U8)
        y = [sbuf("y_%d" % c, [P, PACK, CHUNK], F32) for c in range(CHUNKS)]
        y_grouped = [sbuf("y_grouped_%d" % c, [P, CHUNK, PACK], BF16) for c in range(CHUNKS)]
        y_codes = [sbuf("y_codes_%d" % c, [P, CHUNK], U32) for c in range(CHUNKS)]

        def finish_y(c):
            for h in range(H):
                for u in range(h, PACK, H):
                    nc.vector.scalar_tensor_tensor(
                        out=y[c][:, u, :],
                        in0=xh_rows[c][:, u, :],
                        scalar=og_sb[:, u : u + 1],
                        in1=base_sb[:, u, cols(c)],
                        op0=ALU.mult,
                        op1=ALU.add,
                    )
                nc.sync.dma_start(out=out_rows[:, h::H, cols(c)], in_=y[c][:, h::H, :])

        def quantize_y(c):
            nc.vector.quantize_mx(
                out=y_codes[c][:].bitcast(FP8X4),
                scales=y_scales[:, cols(c)],
                in_=y_grouped[c][:].rearrange("r n u -> r (n u)"),
            )
            nc.sync.dma_start(out=out_words[:, cols(c)], in_=y_codes[c][:].bitcast(I32))

        finish_y(0)
        interleave(y_grouped[0][:], y[0][:])
        finish_y(1)
        quantize_y(0)
        interleave(y_grouped[1][:], y[1][:])
        quantize_y(1)

        for quad in range(P // QUADRANT):
            queue = nc.scalar if quad % 2 else nc.sync
            queue.dma_start(
                out=out_2[0, SCALE_ROWS * quad : SCALE_ROWS * (quad + 1), :].bitcast(I32),
                in_=y_scales[QUADRANT * quad : QUADRANT * quad + SCALE_ROWS, :].bitcast(I32),
            )
